import numpy as np
import ml_dtypes


def mxq(x, axis, fmt="e4m3"):
    dtype, down = {"e4m3": (ml_dtypes.float8_e4m3fn, 7), "e5m2": (ml_dtypes.float8_e5m2, 14)}[fmt]
    v = np.moveaxis(np.asarray(x, np.float32).astype(ml_dtypes.bfloat16).astype(np.float64), axis, -1)
    blocks = v.reshape(v.shape[:-1] + (-1, 32))
    amax = np.abs(blocks).max(-1, keepdims=True)
    byte = np.maximum(np.where(amax > 0, np.frexp(amax)[1] - 1 + 127, 0) - down, 1)
    scale = np.exp2(byte - 127.0)
    codes = (blocks / scale).astype(np.float32).astype(dtype).astype(np.float64)
    return np.moveaxis((codes * scale).reshape(v.shape), -1, axis)


WIDE = False


def mx_kscale(k):
    if not WIDE:
        return np.ones(k)
    levels = np.array([10, -10, 5, -5, 0])
    if k % 512:
        return np.exp2(np.random.permutation(np.resize(levels, k // 32))).repeat(32)
    a = np.empty((k // 512, 16))
    for p in range(k // 512):
        a[p, :8] = np.random.permutation(np.resize(levels, 8))
        for g in range(8):
            far = levels[np.abs(levels - a[p, g]) >= 10]
            a[p, g + 8] = far[np.random.randint(len(far))]
    return np.exp2(a.ravel()).repeat(32)


def f64(x):
    return np.asarray(x).astype(np.float64)


def striped8(idx):
    return np.concatenate([v.reshape(-1, 16).T for v in idx]).astype(np.uint16)


def unstriped8(offs):
    return np.stack([offs[16 * g:16 * g + 16].T.reshape(-1) for g in range(8)]).astype(np.int64)


E2M1 = np.array([0.0, 0.5, 1.0, 1.5, 2.0, 3.0, 4.0, 6.0, -0.0, -0.5, -1.0, -1.5, -2.0, -3.0, -4.0, -6.0])


def pack_weight(w, fmt):
    k, n = w.shape
    w = f64(np.asarray(w, np.float32).astype(ml_dtypes.bfloat16)).reshape(k // 32, 32, n)
    amax = np.abs(w).max(1)
    if fmt == "e4m3":
        byte = np.frexp(amax)[1] - 1 + 127 - 7
    else:
        mant, ex = np.frexp(amax / 6.0)
        byte = np.where(mant > 0.5, ex, ex - 1) + 127
    byte = np.clip(np.where(amax > 0, byte, 1), 1, 254)
    scaled = (w * np.exp2(127.0 - byte)[:, None, :]).reshape(k, n).astype(np.float32)
    by_word = np.ascontiguousarray(scaled.reshape(k // 512, 128, 4, n).transpose(0, 1, 3, 2))
    if fmt == "e4m3":
        words = by_word.astype(ml_dtypes.float8_e4m3fn).view(np.uint8)
    else:
        c = by_word.astype(ml_dtypes.float4_e2m1fn).view(np.uint8) & 0xF
        words = (c[..., 0::2] | (c[..., 1::2] << 4)).reshape(k // 512, 128, 2 * n)
    return np.ascontiguousarray(words), np.ascontiguousarray(byte.astype(np.uint8).reshape(k // 512, 16, n))


def unpack_weight(words, scales, fmt):
    g, _, n = scales.shape
    words = np.ascontiguousarray(words).reshape(g, 128, n, -1)
    if fmt == "e4m3":
        vals = words.view(ml_dtypes.float8_e4m3fn).astype(np.float64)
    else:
        nib = np.empty((g, 128, n, 4), np.uint8)
        nib[..., 0::2] = words & 0xF
        nib[..., 1::2] = words >> 4
        vals = E2M1[nib]
    vals = vals * np.repeat(np.exp2(scales.astype(np.float64) - 127.0), 8, axis=1)[..., None]
    return vals.transpose(0, 1, 3, 2).reshape(g * 512, n)


def silu(v):
    return v / (1.0 + np.exp(-np.maximum(v, -700.0)))


K, M, T, S = 1024, 128, 2048, 1024


def setup_inputs():
    n = np.random.standard_normal
    s = mx_kscale(K)[:, None]
    p_w = pack_weight(n((K, M)) / np.sqrt(K) / s, "e4m3")
    return {
        "xT": (n((K, T)) * s).astype(np.float32),
        "w_words": p_w[0],
        "w_scales": p_w[1],
        "wgt": np.repeat(np.random.uniform(0.5, 2.0, (8, S)), 16, axis=0).astype(np.float32),
        "b": (0.3 * n(128)).astype(np.float32),
        "offs": striped8(np.stack([np.random.permutation(T)[:S] for _ in range(8)])),
    }


def reference(xT, w_words, w_scales, wgt, b, offs):
    idx = unstriped8(offs)
    group = np.arange(K) % 512 // 64
    xg = f64(wgt)[np.arange(K) // 4 % 128] * f64(xT)[np.arange(K)[:, None], idx[group]]
    xT_ = mxq(xg, 0, "e4m3")
    w_ = unpack_weight(w_words, w_scales, "e4m3")
    y = xT_.T @ w_
    return silu(y + f64(b)[None, :])

@@ -1,0 +1,167 @@
+from contextlib import ExitStack
+
+import concourse.mybir as mybir
+from concourse.masks import make_identity
+
+F32 = mybir.dt.float32
+BF16 = mybir.dt.bfloat16
+I32 = mybir.dt.int32
+U32 = mybir.dt.uint32
+U16 = mybir.dt.uint16
+U8 = mybir.dt.uint8
+FP8X4 = mybir.dt.float8_e4m3fn_x4
+MULT = mybir.AluOpType.mult
+ADD = mybir.AluOpType.add
+SILU = mybir.ActivationFunctionType.Silu
+
+K, M, T, S = 1024, 128, 2048, 1024
+P = 128
+PACK = 4
+PASSES = K // (P * PACK)
+FLOPS = 2 * K * M * S
+
+HALF = 512
+SLICES = [(0, 512), (512, 256), (768, 128), (896, 128)]
+
+
+def tile_list_heads_tm_silu_kernel(tc, xT, w_words, w_scales, wgt, b, offs, out):
+    nc = tc.nc
+    with ExitStack() as ctx:
+        keep = ctx.enter_context(tc.tile_pool(name="keep", bufs=1))
+        psum = ctx.enter_context(tc.psum_pool(name="psum", bufs=1))
+
+        offsets = keep.tile([P, S // 16], U16, name="offsets")
+        nc.sync.dma_start(offsets[:], offs)
+
+        rows = xT.rearrange("(a p i) t -> a i p t", p=P, i=PACK)
+        planes = [keep.tile([P, T], F32, name=f"plane{u}") for u in range(PASSES * PACK)]
+        wg = keep.tile([P, S], F32, name="wg")
+        w_codes = keep.tile([P, PASSES, M], U32, name="w_codes", align_bytes=64)
+        w_sc = keep.tile([P, PASSES, M], U8, name="w_sc", align_bytes=64)
+        b_col = keep.tile([P, 1], F32, name="b_col")
+
+        def load_plane(u):
+            nc.sync.dma_start(planes[u][:], rows[u // PACK, u % PACK])
+
+        load_plane(0)
+        for h in range(2):
+            nc.sync.dma_start(wg[:, h * HALF : (h + 1) * HALF], wgt[:, h * HALF : (h + 1) * HALF])
+        load_plane(1)
+        load_plane(2)
+        load_plane(3)
+
+        warm = keep.tile([P, 1], F32, name="warm")
+        nc.vector.memset(warm[:], 0.0)
+        nc.scalar.activation(warm[:], warm[:], SILU)
+        nc.vector.memset(w_sc[:].rearrange("p a n -> p (a n)").bitcast(I32), 0)
+        ident = keep.tile([P, P], F32, name="ident")
+        make_identity(nc, ident[:])
+
+        nc.sync.dma_start(w_codes[:].bitcast(I32), w_words.rearrange("a p n i -> p a (n i)").bitcast(I32))
+        sc_rows = w_scales.bitcast(I32).rearrange("a q n -> q a n")
+        for q in range(4):
+            nc.sync.dma_start(w_sc[32 * q : 32 * q + 4].bitcast(I32), sc_rows[4 * q : 4 * q + 4])
+        nc.sync.dma_start(b_col[:], b.rearrange("(p o) -> p o", o=1))
+        for u in range(4, 8):
+            load_plane(u)
+
+        picked = [keep.tile([P, PACK, S], F32, name=f"picked{a}") for a in range(PASSES)]
+        grouped = [keep.tile([P, S, PACK], BF16, name=f"grouped{a}", align_bytes=64) for a in range(PASSES)]
+        codes = [keep.tile([P, S], U32, name=f"codes{a}", align_bytes=64) for a in range(PASSES)]
+        scales = [keep.tile([P, S], U8, name=f"scales{a}", align_bytes=64) for a in range(PASSES)]
+
+        def gather(u, j0, n):
+            cols = slice(j0, j0 + n)
+            nc.vector.tensor_tensor(
+                picked[u // PACK][:, u % PACK, cols],
+                planes[u][:].indirect(offsets[:, j0 // 16 : (j0 + n) // 16]),
+                wg[:, cols],
+                MULT,
+            )
+
+        def interleave(a, i0, i1, j0, n):
+            cols = slice(j0, j0 + n)
+            nc.scalar.copy(grouped[a][:, cols, i0:i1], picked[a][:, i0:i1, cols].rearrange("p i j -> p j i"))
+
+        def quantise(a, j0, n):
+            cols = slice(j0, j0 + n)
+            nc.vector.quantize_mx(
+                out=codes[a][:, cols].bitcast(FP8X4),
+                scales=scales[a][:, cols],
+                in_=grouped[a][:, cols, :].rearrange("p j i -> p (j i)"),
+            )
+
+        bias_ps = psum.tile([P, P], F32, name="bias_ps")
+        nc.tensor.transpose(bias_ps[:], b_col[:].to_broadcast([P, P]), ident[:])
+        bias = keep.tile([P, P], F32, name="bias")
+        nc.scalar.copy(bias[:], bias_ps[:])
+
+        for u in range(4):
+            gather(u, 0, HALF)
+            gather(u, HALF, HALF)
+        interleave(0, 0, 4, 0, HALF)
+        interleave(0, 0, 4, HALF, HALF)
+        gather(4, 0, HALF)
+        gather(4, HALF, HALF)
+        gather(5, 0, HALF)
+        gather(5, HALF, HALF)
+        quantise(0, 0, S)
+        interleave(1, 0, 2, 0, HALF)
+        interleave(1, 0, 2, HALF, HALF)
+
+        def project_wide(j0, n):
+            acc = psum.tile([P, n], F32, name=f"acc{j0}")
+            for a in range(PASSES):
+                nc.tensor.matmul_mx(
+                    out=acc[:],
+                    lhsT=w_codes[:, a, :].bitcast(FP8X4),
+                    lhsT_scale=w_sc[:, a, :],
+                    rhs=codes[a][:, j0 : j0 + n].bitcast(FP8X4),
+                    rhs_scale=scales[a][:, j0 : j0 + n],
+                    start=(a == 0),
+                    stop=(a == PASSES - 1),
+                )
+            y = keep.tile([P, n], F32, name=f"y{j0}")
+            nc.scalar.activation(y[:], acc[:], SILU, bias=b_col[:])
+            turned = psum.tile([P, n // P, P], F32, name=f"turned{j0}")
+            for c in range(n // P):
+                nc.tensor.transpose(turned[:, c, :], y[:, c * P : (c + 1) * P], ident[:])
+            res = keep.tile([P, n // P, P], F32, name=f"res{j0}")
+            nc.scalar.copy(res[:], turned[:])
+            nc.sync.dma_start(out[j0 : j0 + n, :].rearrange("(c p) n -> p c n", p=P), res[:])
+
+        def project(j0, n):
+            acc = psum.tile([P, n // P, P], F32, name=f"acc{j0}")
+            for c in range(n // P):
+                cols = slice(j0 + c * P, j0 + (c + 1) * P)
+                for a in range(PASSES):
+                    nc.tensor.matmul_mx(
+                        out=acc[:, c, :],
+                        lhsT=codes[a][:, cols].bitcast(FP8X4),
+                        lhsT_scale=scales[a][:, cols],
+                        rhs=w_codes[:, a, :].bitcast(FP8X4),
+                        rhs_scale=w_sc[:, a, :],
+                        start=(a == 0),
+                        stop=(a == PASSES - 1),
+                    )
+            y = keep.tile([P, n // P, P], F32, name=f"y{j0}")
+            nc.vector.tensor_tensor(y[:], acc[:], bias[:].unsqueeze(1).to_broadcast([P, n // P, P]), ADD)
+            res = keep.tile([P, n // P, P], F32, name=f"res{j0}")
+            nc.scalar.activation(res[:], y[:], SILU)
+            nc.sync.dma_start(out[j0 : j0 + n, :].rearrange("(c p) n -> p c n", p=P), res[:])
+
+        def finish(s):
+            j0, n = SLICES[s]
+            quantise(1, j0, n)
+            if s == 0:
+                project_wide(j0, n)
+            else:
+                project(j0, n)
+
+        for s, (j0, n) in enumerate(SLICES):
+            gather(6, j0, n)
+            gather(7, j0, n)
+            interleave(1, 2, 4, j0, n)
+            if s > 0:
+                finish(s - 1)
+        finish(len(SLICES) - 1)

@@ -21,7 +21,7 @@ PASSES = K // (P * PACK)
 FLOPS = 2 * K * M * S
 
 HALF = 512
-SLICES = [(0, 512), (512, 256), (768, 128), (896, 128)]
+SLICES = [[(0, 512)], [(512, 256), (768, 128), (896, 128)]]
 
 
 def tile_list_heads_tm_silu_kernel(tc, xT, w_words, w_scales, wgt, b, offs, out):
@@ -46,9 +46,8 @@ def tile_list_heads_tm_silu_kernel(tc, xT, w_words, w_scales, wgt, b, offs, out)
         load_plane(0)
         for h in range(2):
             nc.sync.dma_start(wg[:, h * HALF : (h + 1) * HALF], wgt[:, h * HALF : (h + 1) * HALF])
-        load_plane(1)
-        load_plane(2)
-        load_plane(3)
+        for u in range(1, 7):
+            load_plane(u)
 
         warm = keep.tile([P, 1], F32, name="warm")
         nc.vector.memset(warm[:], 0.0)
@@ -62,26 +61,43 @@ def tile_list_heads_tm_silu_kernel(tc, xT, w_words, w_scales, wgt, b, offs, out)
         for q in range(4):
             nc.sync.dma_start(w_sc[32 * q : 32 * q + 4].bitcast(I32), sc_rows[4 * q : 4 * q + 4])
         nc.sync.dma_start(b_col[:], b.rearrange("(p o) -> p o", o=1))
-        for u in range(4, 8):
-            load_plane(u)
+        load_plane(7)
 
-        picked = [keep.tile([P, PACK, S], F32, name=f"picked{a}") for a in range(PASSES)]
         grouped = [keep.tile([P, S, PACK], BF16, name=f"grouped{a}", align_bytes=64) for a in range(PASSES)]
         codes = [keep.tile([P, S], U32, name=f"codes{a}", align_bytes=64) for a in range(PASSES)]
         scales = [keep.tile([P, S], U8, name=f"scales{a}", align_bytes=64) for a in range(PASSES)]
 
-        def gather(u, j0, n):
-            cols = slice(j0, j0 + n)
+        def picked_tile(u0, count, j0, n):
+            return keep.tile([P, count, n], F32, name=f"picked{u0}_{j0}")
+
+        def gather(picked, u, u0, j0, n):
             nc.vector.tensor_tensor(
-                picked[u // PACK][:, u % PACK, cols],
+                picked[:, u - u0, :],
                 planes[u][:].indirect(offsets[:, j0 // 16 : (j0 + n) // 16]),
-                wg[:, cols],
+                wg[:, j0 : j0 + n],
                 MULT,
             )
 
-        def interleave(a, i0, i1, j0, n):
-            cols = slice(j0, j0 + n)
-            nc.scalar.copy(grouped[a][:, cols, i0:i1], picked[a][:, i0:i1, cols].rearrange("p i j -> p j i"))
+        def interleave(picked, u0, count, j0, n):
+            i0 = u0 % PACK
+            nc.scalar.copy(
+                grouped[u0 // PACK][:, j0 : j0 + n, i0 : i0 + count], picked[:].rearrange("p i j -> p j i")
+            )
+
+        def gather_part(picked, u, u0, base, j0, n):
+            nc.vector.tensor_tensor(
+                picked[:, u - u0, j0 - base : j0 - base + n],
+                planes[u][:].indirect(offsets[:, j0 // 16 : (j0 + n) // 16]),
+                wg[:, j0 : j0 + n],
+                MULT,
+            )
+
+        def interleave_part(picked, u0, count, base, j0, n):
+            i0 = u0 % PACK
+            nc.scalar.copy(
+                grouped[u0 // PACK][:, j0 : j0 + n, i0 : i0 + count],
+                picked[:, :, j0 - base : j0 - base + n].rearrange("p i j -> p j i"),
+            )
 
         def quantise(a, j0, n):
             cols = slice(j0, j0 + n)
@@ -96,18 +112,20 @@ def tile_list_heads_tm_silu_kernel(tc, xT, w_words, w_scales, wgt, b, offs, out)
         bias = keep.tile([P, P], F32, name="bias")
         nc.scalar.copy(bias[:], bias_ps[:])
 
+        halves = [(0, HALF), (HALF, HALF)]
+        first = [picked_tile(0, 4, j0, n) for j0, n in halves]
         for u in range(4):
-            gather(u, 0, HALF)
-            gather(u, HALF, HALF)
-        interleave(0, 0, 4, 0, HALF)
-        interleave(0, 0, 4, HALF, HALF)
-        gather(4, 0, HALF)
-        gather(4, HALF, HALF)
-        gather(5, 0, HALF)
-        gather(5, HALF, HALF)
+            for h, (j0, n) in enumerate(halves):
+                gather(first[h], u, 0, j0, n)
+        for h, (j0, n) in enumerate(halves):
+            interleave(first[h], 0, 4, j0, n)
+        second = [picked_tile(4, 2, j0, n) for j0, n in halves]
+        for u in (4, 5):
+            for h, (j0, n) in enumerate(halves):
+                gather(second[h], u, 4, j0, n)
         quantise(0, 0, S)
-        interleave(1, 0, 2, 0, HALF)
-        interleave(1, 0, 2, HALF, HALF)
+        for h, (j0, n) in enumerate(halves):
+            interleave(second[h], 4, 2, j0, n)
 
         def project_wide(j0, n):
             acc = psum.tile([P, n], F32, name=f"acc{j0}")
@@ -150,18 +168,17 @@ def tile_list_heads_tm_silu_kernel(tc, xT, w_words, w_scales, wgt, b, offs, out)
             nc.scalar.activation(res[:], y[:], SILU)
             nc.sync.dma_start(out[j0 : j0 + n, :].rearrange("(c p) n -> p c n", p=P), res[:])
 
-        def finish(s):
-            j0, n = SLICES[s]
+        def finish(j0, n):
             quantise(1, j0, n)
-            if s == 0:
+            if j0 in ():
                 project_wide(j0, n)
             else:
                 project(j0, n)
 
-        for s, (j0, n) in enumerate(SLICES):
-            gather(6, j0, n)
-            gather(7, j0, n)
-            interleave(1, 2, 4, j0, n)
-            if s > 0:
-                finish(s - 1)
-        finish(len(SLICES) - 1)
+        last = [picked_tile(6, 2, j0, n) for j0, n in halves]
+        for h, (j0, n) in enumerate(halves):
+            gather(last[h], 6, 6, j0, n)
+            for s0, sn in SLICES[h]:
+                gather_part(last[h], 7, 6, j0, s0, sn)
+                interleave_part(last[h], 6, 2, j0, s0, sn)
+                finish(s0, sn)

@@ -15,13 +15,21 @@ ADD = mybir.AluOpType.add
 SILU = mybir.ActivationFunctionType.Silu
 
 K, M, T, S = 1024, 128, 2048, 1024
+FLOPS = 2 * K * M * S
+
 P = 128
 PACK = 4
 PASSES = K // (P * PACK)
-FLOPS = 2 * K * M * S
+PLANES = PASSES * PACK
+LANES = 16
 
-HALF = 512
-SLICES = [[(0, 512)], [(512, 256), (768, 128), (896, 128)]]
+HALVES = [(0, 512), (512, 512)]
+
+TURNED_SLICES = [(0, 256), (256, 256)]
+DIRECT_SLICES = [(512, 256), (768, 128), (896, 128)]
+LAST_SLICE = DIRECT_SLICES[-1]
+
+PLANE_6_PIECES = [(512, 256), (768, 256)]
 
 
 def tile_list_heads_tm_silu_kernel(tc, xT, w_words, w_scales, wgt, b, offs, out):
@@ -30,155 +38,150 @@ def tile_list_heads_tm_silu_kernel(tc, xT, w_words, w_scales, wgt, b, offs, out)
         keep = ctx.enter_context(tc.tile_pool(name="keep", bufs=1))
         psum = ctx.enter_context(tc.psum_pool(name="psum", bufs=1))
 
-        offsets = keep.tile([P, S // 16], U16, name="offsets")
+        offsets = keep.tile([P, S // LANES], U16, name="offsets")
         nc.sync.dma_start(offsets[:], offs)
 
-        rows = xT.rearrange("(a p i) t -> a i p t", p=P, i=PACK)
-        planes = [keep.tile([P, T], F32, name=f"plane{u}") for u in range(PASSES * PACK)]
-        wg = keep.tile([P, S], F32, name="wg")
+        plane_rows = xT.rearrange("(a p i) t -> a i p t", p=P, i=PACK)
+        planes = [keep.tile([P, T], F32, name=f"plane{u}") for u in range(PLANES)]
+        token_weights = keep.tile([P, S], F32, name="token_weights")
         w_codes = keep.tile([P, PASSES, M], U32, name="w_codes", align_bytes=64)
-        w_sc = keep.tile([P, PASSES, M], U8, name="w_sc", align_bytes=64)
-        b_col = keep.tile([P, 1], F32, name="b_col")
+        w_scale_rows = keep.tile([P, PASSES, M], U8, name="w_scale_rows", align_bytes=64)
+        b_column = keep.tile([P, 1], F32, name="b_column")
 
         def load_plane(u):
-            nc.sync.dma_start(planes[u][:], rows[u // PACK, u % PACK])
+            nc.sync.dma_start(planes[u][:], plane_rows[u // PACK, u % PACK])
 
         load_plane(0)
-        for h in range(2):
-            nc.sync.dma_start(wg[:, h * HALF : (h + 1) * HALF], wgt[:, h * HALF : (h + 1) * HALF])
-        for u in range(1, 7):
+        for j0, n in HALVES:
+            nc.sync.dma_start(token_weights[:, j0 : j0 + n], wgt[:, j0 : j0 + n])
+        for u in range(1, 6):
             load_plane(u)
 
-        warm = keep.tile([P, 1], F32, name="warm")
-        nc.vector.memset(warm[:], 0.0)
-        nc.scalar.activation(warm[:], warm[:], SILU)
-        nc.vector.memset(w_sc[:].rearrange("p a n -> p (a n)").bitcast(I32), 0)
-        ident = keep.tile([P, P], F32, name="ident")
-        make_identity(nc, ident[:])
+        warm_up = keep.tile([P, 1], F32, name="warm_up")
+        nc.vector.memset(warm_up[:], 0.0)
+        nc.scalar.activation(warm_up[:], warm_up[:], SILU)
+        nc.vector.memset(w_scale_rows[:].rearrange("p a n -> p (a n)").bitcast(I32), 0)
+        identity = keep.tile([P, P], F32, name="identity")
+        make_identity(nc, identity[:])
 
         nc.sync.dma_start(w_codes[:].bitcast(I32), w_words.rearrange("a p n i -> p a (n i)").bitcast(I32))
-        sc_rows = w_scales.bitcast(I32).rearrange("a q n -> q a n")
-        for q in range(4):
-            nc.sync.dma_start(w_sc[32 * q : 32 * q + 4].bitcast(I32), sc_rows[4 * q : 4 * q + 4])
-        nc.sync.dma_start(b_col[:], b.rearrange("(p o) -> p o", o=1))
+        scale_source = w_scales.bitcast(I32).rearrange("a q n -> q a n")
+        for quadrant in range(4):
+            nc.sync.dma_start(
+                w_scale_rows[32 * quadrant : 32 * quadrant + 4].bitcast(I32),
+                scale_source[4 * quadrant : 4 * quadrant + 4],
+            )
+        nc.sync.dma_start(b_column[:], b.rearrange("(p o) -> p o", o=1))
+        load_plane(6)
         load_plane(7)
 
         grouped = [keep.tile([P, S, PACK], BF16, name=f"grouped{a}", align_bytes=64) for a in range(PASSES)]
         codes = [keep.tile([P, S], U32, name=f"codes{a}", align_bytes=64) for a in range(PASSES)]
         scales = [keep.tile([P, S], U8, name=f"scales{a}", align_bytes=64) for a in range(PASSES)]
 
-        def picked_tile(u0, count, j0, n):
-            return keep.tile([P, count, n], F32, name=f"picked{u0}_{j0}")
+        def picked_tiles(u, count):
+            return [keep.tile([P, count, n], F32, name=f"picked{u}_{j0}") for j0, n in HALVES]
 
-        def gather(picked, u, u0, j0, n):
+        def gather(picked, u, j0, n):
             nc.vector.tensor_tensor(
-                picked[:, u - u0, :],
-                planes[u][:].indirect(offsets[:, j0 // 16 : (j0 + n) // 16]),
-                wg[:, j0 : j0 + n],
+                picked,
+                planes[u][:].indirect(offsets[:, j0 // LANES : (j0 + n) // LANES]),
+                token_weights[:, j0 : j0 + n],
                 MULT,
             )
 
-        def interleave(picked, u0, count, j0, n):
-            i0 = u0 % PACK
-            nc.scalar.copy(
-                grouped[u0 // PACK][:, j0 : j0 + n, i0 : i0 + count], picked[:].rearrange("p i j -> p j i")
-            )
-
-        def gather_part(picked, u, u0, base, j0, n):
-            nc.vector.tensor_tensor(
-                picked[:, u - u0, j0 - base : j0 - base + n],
-                planes[u][:].indirect(offsets[:, j0 // 16 : (j0 + n) // 16]),
-                wg[:, j0 : j0 + n],
-                MULT,
-            )
-
-        def interleave_part(picked, u0, count, base, j0, n):
-            i0 = u0 % PACK
-            nc.scalar.copy(
-                grouped[u0 // PACK][:, j0 : j0 + n, i0 : i0 + count],
-                picked[:, :, j0 - base : j0 - base + n].rearrange("p i j -> p j i"),
+        def interleave(copy, picked, u, j0, n):
+            i0 = u % PACK
+            copy(
+                grouped[u // PACK][:, j0 : j0 + n, i0 : i0 + picked.shape[1]],
+                picked.rearrange("p i j -> p j i"),
             )
 
         def quantise(a, j0, n):
-            cols = slice(j0, j0 + n)
             nc.vector.quantize_mx(
-                out=codes[a][:, cols].bitcast(FP8X4),
-                scales=scales[a][:, cols],
-                in_=grouped[a][:, cols, :].rearrange("p j i -> p (j i)"),
+                out=codes[a][:, j0 : j0 + n].bitcast(FP8X4),
+                scales=scales[a][:, j0 : j0 + n],
+                in_=grouped[a][:, j0 : j0 + n, :].rearrange("p j i -> p (j i)"),
             )
 
-        bias_ps = psum.tile([P, P], F32, name="bias_ps")
-        nc.tensor.transpose(bias_ps[:], b_col[:].to_broadcast([P, P]), ident[:])
-        bias = keep.tile([P, P], F32, name="bias")
-        nc.scalar.copy(bias[:], bias_ps[:])
-
-        halves = [(0, HALF), (HALF, HALF)]
-        first = [picked_tile(0, 4, j0, n) for j0, n in halves]
-        for u in range(4):
-            for h, (j0, n) in enumerate(halves):
-                gather(first[h], u, 0, j0, n)
-        for h, (j0, n) in enumerate(halves):
-            interleave(first[h], 0, 4, j0, n)
-        second = [picked_tile(4, 2, j0, n) for j0, n in halves]
-        for u in (4, 5):
-            for h, (j0, n) in enumerate(halves):
-                gather(second[h], u, 4, j0, n)
-        quantise(0, 0, S)
-        for h, (j0, n) in enumerate(halves):
-            interleave(second[h], 4, 2, j0, n)
-
-        def project_wide(j0, n):
+        def project_turned(j0, n):
             acc = psum.tile([P, n], F32, name=f"acc{j0}")
             for a in range(PASSES):
                 nc.tensor.matmul_mx(
                     out=acc[:],
                     lhsT=w_codes[:, a, :].bitcast(FP8X4),
-                    lhsT_scale=w_sc[:, a, :],
+                    lhsT_scale=w_scale_rows[:, a, :],
                     rhs=codes[a][:, j0 : j0 + n].bitcast(FP8X4),
                     rhs_scale=scales[a][:, j0 : j0 + n],
                     start=(a == 0),
                     stop=(a == PASSES - 1),
                 )
-            y = keep.tile([P, n], F32, name=f"y{j0}")
-            nc.scalar.activation(y[:], acc[:], SILU, bias=b_col[:])
+            columns = keep.tile([P, n], F32, name=f"columns{j0}")
+            nc.scalar.activation(columns[:], acc[:], SILU, bias=b_column[:])
             turned = psum.tile([P, n // P, P], F32, name=f"turned{j0}")
             for c in range(n // P):
-                nc.tensor.transpose(turned[:, c, :], y[:, c * P : (c + 1) * P], ident[:])
-            res = keep.tile([P, n // P, P], F32, name=f"res{j0}")
-            nc.scalar.copy(res[:], turned[:])
-            nc.sync.dma_start(out[j0 : j0 + n, :].rearrange("(c p) n -> p c n", p=P), res[:])
+                nc.tensor.transpose(turned[:, c, :], columns[:, c * P : (c + 1) * P], identity[:])
+            rows = keep.tile([P, n // P, P], F32, name=f"rows{j0}")
+            nc.scalar.copy(rows[:], turned[:])
+            nc.sync.dma_start(out[j0 : j0 + n, :].rearrange("(c p) n -> p c n", p=P), rows[:])
 
-        def project(j0, n):
+        def project_direct(store, j0, n):
             acc = psum.tile([P, n // P, P], F32, name=f"acc{j0}")
             for c in range(n // P):
-                cols = slice(j0 + c * P, j0 + (c + 1) * P)
+                tokens = slice(j0 + c * P, j0 + (c + 1) * P)
                 for a in range(PASSES):
                     nc.tensor.matmul_mx(
                         out=acc[:, c, :],
-                        lhsT=codes[a][:, cols].bitcast(FP8X4),
-                        lhsT_scale=scales[a][:, cols],
+                        lhsT=codes[a][:, tokens].bitcast(FP8X4),
+                        lhsT_scale=scales[a][:, tokens],
                         rhs=w_codes[:, a, :].bitcast(FP8X4),
-                        rhs_scale=w_sc[:, a, :],
+                        rhs_scale=w_scale_rows[:, a, :],
                         start=(a == 0),
                         stop=(a == PASSES - 1),
                     )
-            y = keep.tile([P, n // P, P], F32, name=f"y{j0}")
-            nc.vector.tensor_tensor(y[:], acc[:], bias[:].unsqueeze(1).to_broadcast([P, n // P, P]), ADD)
-            res = keep.tile([P, n // P, P], F32, name=f"res{j0}")
-            nc.scalar.activation(res[:], y[:], SILU)
-            nc.sync.dma_start(out[j0 : j0 + n, :].rearrange("(c p) n -> p c n", p=P), res[:])
+            biased = keep.tile([P, n // P, P], F32, name=f"biased{j0}")
+            nc.vector.tensor_tensor(biased[:], acc[:], b_rows[:].unsqueeze(1).to_broadcast([P, n // P, P]), ADD)
+            rows = keep.tile([P, n // P, P], F32, name=f"rows{j0}")
+            nc.scalar.activation(rows[:], biased[:], SILU)
+            store(out[j0 : j0 + n, :].rearrange("(c p) n -> p c n", p=P), rows[:])
 
-        def finish(j0, n):
+        b_turned = psum.tile([P, P], F32, name="b_turned")
+        nc.tensor.transpose(b_turned[:], b_column[:].to_broadcast([P, P]), identity[:])
+        b_rows = keep.tile([P, P], F32, name="b_rows")
+        nc.scalar.copy(b_rows[:], b_turned[:])
+
+        picked = picked_tiles(0, 4)
+        for u in range(4):
+            for h, (j0, n) in enumerate(HALVES):
+                gather(picked[h][:, u, :], u, j0, n)
+        for h, (j0, n) in enumerate(HALVES):
+            interleave(nc.scalar.copy, picked[h][:], 0, j0, n)
+
+        picked = picked_tiles(4, 2)
+        for u in (4, 5):
+            for h, (j0, n) in enumerate(HALVES):
+                gather(picked[h][:, u - 4, :], u, j0, n)
+        for h, (j0, n) in enumerate(HALVES):
+            interleave(nc.scalar.copy, picked[h][:], 4, j0, n)
+
+        front, back = picked_tiles(6, 2)
+        gather(front[:, 0, :], 6, 0, 512)
+        for j0, n in TURNED_SLICES:
+            gather(front[:, 1, j0 : j0 + n], 7, j0, n)
+            interleave(nc.scalar.copy, front[:, :, j0 : j0 + n], 6, j0, n)
+            if j0 == 0:
+                for first, tokens in HALVES:
+                    quantise(0, first, tokens)
             quantise(1, j0, n)
-            if j0 in ():
-                project_wide(j0, n)
-            else:
-                project(j0, n)
+            project_turned(j0, n)
 
-        last = [picked_tile(6, 2, j0, n) for j0, n in halves]
-        for h, (j0, n) in enumerate(halves):
-            gather(last[h], 6, 6, j0, n)
-            for s0, sn in SLICES[h]:
-                gather_part(last[h], 7, 6, j0, s0, sn)
-                interleave_part(last[h], 6, 2, j0, s0, sn)
-                finish(s0, sn)
+        for j0, n in PLANE_6_PIECES:
+            gather(back[:, 0, j0 - 512 : j0 - 512 + n], 6, j0, n)
+        for j0, n in DIRECT_SLICES:
+            is_last = (j0, n) == LAST_SLICE
+            gather(back[:, 1, j0 - 512 : j0 - 512 + n], 7, j0, n)
+            copy = nc.vector.tensor_copy if is_last else nc.scalar.copy
+            store = nc.scalar.dma_start if is_last else nc.sync.dma_start
+            interleave(copy, back[:, :, j0 - 512 : j0 - 512 + n], 6, j0, n)
+            quantise(1, j0, n)
+            project_direct(store, j0, n)

from contextlib import ExitStack

import concourse.mybir as mybir
from concourse.masks import make_identity

F32 = mybir.dt.float32
BF16 = mybir.dt.bfloat16
I32 = mybir.dt.int32
U32 = mybir.dt.uint32
U16 = mybir.dt.uint16
U8 = mybir.dt.uint8
FP8X4 = mybir.dt.float8_e4m3fn_x4
MULT = mybir.AluOpType.mult
ADD = mybir.AluOpType.add
SILU = mybir.ActivationFunctionType.Silu

K, M, T, S = 1024, 128, 2048, 1024
FLOPS = 2 * K * M * S

P = 128
PACK = 4
PASSES = K // (P * PACK)
PLANES = PASSES * PACK
LANES = 16

HALVES = [(0, 512), (512, 512)]

TURNED_SLICES = [(0, 256), (256, 256)]
DIRECT_SLICES = [(512, 256), (768, 128), (896, 128)]
LAST_SLICE = DIRECT_SLICES[-1]

PLANE_6_PIECES = [(512, 256), (768, 256)]


def tile_list_heads_tm_silu_kernel(tc, xT, w_words, w_scales, wgt, b, offs, out):
    nc = tc.nc
    with ExitStack() as ctx:
        keep = ctx.enter_context(tc.tile_pool(name="keep", bufs=1))
        psum = ctx.enter_context(tc.psum_pool(name="psum", bufs=1))

        offsets = keep.tile([P, S // LANES], U16, name="offsets")
        nc.sync.dma_start(offsets[:], offs)

        plane_rows = xT.rearrange("(a p i) t -> a i p t", p=P, i=PACK)
        planes = [keep.tile([P, T], F32, name=f"plane{u}") for u in range(PLANES)]
        token_weights = keep.tile([P, S], F32, name="token_weights")
        w_codes = keep.tile([P, PASSES, M], U32, name="w_codes", align_bytes=64)
        w_scale_rows = keep.tile([P, PASSES, M], U8, name="w_scale_rows", align_bytes=64)
        b_column = keep.tile([P, 1], F32, name="b_column")

        def load_plane(u):
            nc.sync.dma_start(planes[u][:], plane_rows[u // PACK, u % PACK])

        load_plane(0)
        for j0, n in HALVES:
            nc.sync.dma_start(token_weights[:, j0 : j0 + n], wgt[:, j0 : j0 + n])
        for u in range(1, 6):
            load_plane(u)

        warm_up = keep.tile([P, 1], F32, name="warm_up")
        nc.vector.memset(warm_up[:], 0.0)
        nc.scalar.activation(warm_up[:], warm_up[:], SILU)
        nc.vector.memset(w_scale_rows[:].rearrange("p a n -> p (a n)").bitcast(I32), 0)
        identity = keep.tile([P, P], F32, name="identity")
        make_identity(nc, identity[:])

        nc.sync.dma_start(w_codes[:].bitcast(I32), w_words.rearrange("a p n i -> p a (n i)").bitcast(I32))
        scale_source = w_scales.bitcast(I32).rearrange("a q n -> q a n")
        for quadrant in range(4):
            nc.sync.dma_start(
                w_scale_rows[32 * quadrant : 32 * quadrant + 4].bitcast(I32),
                scale_source[4 * quadrant : 4 * quadrant + 4],
            )
        nc.sync.dma_start(b_column[:], b.rearrange("(p o) -> p o", o=1))
        load_plane(6)
        load_plane(7)

        grouped = [keep.tile([P, S, PACK], BF16, name=f"grouped{a}", align_bytes=64) for a in range(PASSES)]
        codes = [keep.tile([P, S], U32, name=f"codes{a}", align_bytes=64) for a in range(PASSES)]
        scales = [keep.tile([P, S], U8, name=f"scales{a}", align_bytes=64) for a in range(PASSES)]

        def picked_tiles(u, count):
            return [keep.tile([P, count, n], F32, name=f"picked{u}_{j0}") for j0, n in HALVES]

        def gather(picked, u, j0, n):
            nc.vector.tensor_tensor(
                picked,
                planes[u][:].indirect(offsets[:, j0 // LANES : (j0 + n) // LANES]),
                token_weights[:, j0 : j0 + n],
                MULT,
            )

        def interleave(copy, picked, u, j0, n):
            i0 = u % PACK
            copy(
                grouped[u // PACK][:, j0 : j0 + n, i0 : i0 + picked.shape[1]],
                picked.rearrange("p i j -> p j i"),
            )

        def quantise(a, j0, n):
            nc.vector.quantize_mx(
                out=codes[a][:, j0 : j0 + n].bitcast(FP8X4),
                scales=scales[a][:, j0 : j0 + n],
                in_=grouped[a][:, j0 : j0 + n, :].rearrange("p j i -> p (j i)"),
            )

        def project_turned(j0, n):
            acc = psum.tile([P, n], F32, name=f"acc{j0}")
            for a in range(PASSES):
                nc.tensor.matmul_mx(
                    out=acc[:],
                    lhsT=w_codes[:, a, :].bitcast(FP8X4),
                    lhsT_scale=w_scale_rows[:, a, :],
                    rhs=codes[a][:, j0 : j0 + n].bitcast(FP8X4),
                    rhs_scale=scales[a][:, j0 : j0 + n],
                    start=(a == 0),
                    stop=(a == PASSES - 1),
                )
            columns = keep.tile([P, n], F32, name=f"columns{j0}")
            nc.scalar.activation(columns[:], acc[:], SILU, bias=b_column[:])
            turned = psum.tile([P, n // P, P], F32, name=f"turned{j0}")
            for c in range(n // P):
                nc.tensor.transpose(turned[:, c, :], columns[:, c * P : (c + 1) * P], identity[:])
            rows = keep.tile([P, n // P, P], F32, name=f"rows{j0}")
            nc.scalar.copy(rows[:], turned[:])
            nc.sync.dma_start(out[j0 : j0 + n, :].rearrange("(c p) n -> p c n", p=P), rows[:])

        def project_direct(store, j0, n):
            acc = psum.tile([P, n // P, P], F32, name=f"acc{j0}")
            for c in range(n // P):
                tokens = slice(j0 + c * P, j0 + (c + 1) * P)
                for a in range(PASSES):
                    nc.tensor.matmul_mx(
                        out=acc[:, c, :],
                        lhsT=codes[a][:, tokens].bitcast(FP8X4),
                        lhsT_scale=scales[a][:, tokens],
                        rhs=w_codes[:, a, :].bitcast(FP8X4),
                        rhs_scale=w_scale_rows[:, a, :],
                        start=(a == 0),
                        stop=(a == PASSES - 1),
                    )
            biased = keep.tile([P, n // P, P], F32, name=f"biased{j0}")
            nc.vector.tensor_tensor(biased[:], acc[:], b_rows[:].unsqueeze(1).to_broadcast([P, n // P, P]), ADD)
            rows = keep.tile([P, n // P, P], F32, name=f"rows{j0}")
            nc.scalar.activation(rows[:], biased[:], SILU)
            store(out[j0 : j0 + n, :].rearrange("(c p) n -> p c n", p=P), rows[:])

        b_turned = psum.tile([P, P], F32, name="b_turned")
        nc.tensor.transpose(b_turned[:], b_column[:].to_broadcast([P, P]), identity[:])
        b_rows = keep.tile([P, P], F32, name="b_rows")
        nc.scalar.copy(b_rows[:], b_turned[:])

        picked = picked_tiles(0, 4)
        for u in range(4):
            for h, (j0, n) in enumerate(HALVES):
                gather(picked[h][:, u, :], u, j0, n)
        for h, (j0, n) in enumerate(HALVES):
            interleave(nc.scalar.copy, picked[h][:], 0, j0, n)

        picked = picked_tiles(4, 2)
        for u in (4, 5):
            for h, (j0, n) in enumerate(HALVES):
                gather(picked[h][:, u - 4, :], u, j0, n)
        for h, (j0, n) in enumerate(HALVES):
            interleave(nc.scalar.copy, picked[h][:], 4, j0, n)

        front, back = picked_tiles(6, 2)
        gather(front[:, 0, :], 6, 0, 512)
        for j0, n in TURNED_SLICES:
            gather(front[:, 1, j0 : j0 + n], 7, j0, n)
            interleave(nc.scalar.copy, front[:, :, j0 : j0 + n], 6, j0, n)
            if j0 == 0:
                for first, tokens in HALVES:
                    quantise(0, first, tokens)
            quantise(1, j0, n)
            project_turned(j0, n)

        for j0, n in PLANE_6_PIECES:
            gather(back[:, 0, j0 - 512 : j0 - 512 + n], 6, j0, n)
        for j0, n in DIRECT_SLICES:
            is_last = (j0, n) == LAST_SLICE
            gather(back[:, 1, j0 - 512 : j0 - 512 + n], 7, j0, n)
            copy = nc.vector.tensor_copy if is_last else nc.scalar.copy
            store = nc.scalar.dma_start if is_last else nc.sync.dma_start
            interleave(copy, back[:, :, j0 - 512 : j0 - 512 + n], 6, j0, n)
            quantise(1, j0, n)
            project_direct(store, j0, n)
